import numpy as np
import ml_dtypes


def mxq(x, axis, fmt="e4m3"):
    dtype, down = {"e4m3": (ml_dtypes.float8_e4m3fn, 7), "e5m2": (ml_dtypes.float8_e5m2, 14)}[fmt]
    v = np.moveaxis(np.asarray(x, np.float32).astype(ml_dtypes.bfloat16).astype(np.float64), axis, -1)
    blocks = v.reshape(v.shape[:-1] + (-1, 32))
    amax = np.abs(blocks).max(-1, keepdims=True)
    byte = np.maximum(np.where(amax > 0, np.frexp(amax)[1] - 1 + 127, 0) - down, 1)
    scale = np.exp2(byte - 127.0)
    codes = (blocks / scale).astype(np.float32).astype(dtype).astype(np.float64)
    return np.moveaxis((codes * scale).reshape(v.shape), -1, axis)


WIDE = False


def mx_kscale(k):
    if not WIDE:
        return np.ones(k)
    levels = np.array([10, -10, 5, -5, 0])
    if k % 512:
        return np.exp2(np.random.permutation(np.resize(levels, k // 32))).repeat(32)
    a = np.empty((k // 512, 16))
    for p in range(k // 512):
        a[p, :8] = np.random.permutation(np.resize(levels, 8))
        for g in range(8):
            far = levels[np.abs(levels - a[p, g]) >= 10]
            a[p, g + 8] = far[np.random.randint(len(far))]
    return np.exp2(a.ravel()).repeat(32)


def f64(x):
    return np.asarray(x).astype(np.float64)


def striped(idx):
    return np.tile(idx.reshape(-1, 16).T, (8, 1)).astype(np.uint16)


def unstriped(offs):
    return offs[:16].T.reshape(-1).astype(np.int64)


def pack_weight(w):
    k, n = w.shape
    w = f64(np.asarray(w, np.float32).astype(ml_dtypes.bfloat16)).reshape(k // 32, 32, n)
    amax = np.abs(w).max(1)
    byte = np.clip(np.where(amax > 0, np.frexp(amax)[1] - 1 + 127 - 7, 1), 1, 254)
    scaled = (w * np.exp2(127.0 - byte)[:, None, :]).reshape(k, n).astype(np.float32)
    words = np.ascontiguousarray(scaled.reshape(k // 512, 128, 4, n).transpose(0, 1, 3, 2)).astype(ml_dtypes.float8_e4m3fn).view(np.uint8)
    return words, np.ascontiguousarray(byte.astype(np.uint8).reshape(k // 512, 16, n))


def unpack_weight(words, scales):
    g, p, n, _ = words.shape
    vals = np.ascontiguousarray(words).view(ml_dtypes.float8_e4m3fn).astype(np.float64) * np.repeat(np.exp2(scales.astype(np.float64) - 127.0), 8, axis=1)[..., None]
    return vals.transpose(0, 1, 3, 2).reshape(g * 512, n)


def sigmoid(v):
    return 1.0 / (1.0 + np.exp(-np.maximum(v, -700.0)))

def planes(y):
    n, m = y.shape
    v = y.astype(np.float32).astype(ml_dtypes.bfloat16).astype(np.float64).reshape(n // 32, 32, m)
    top = np.abs(v).max(1)
    byte = np.clip(np.where(top > 0, np.frexp(top)[1] - 1 + 127 - 7, 1), 1, 254)
    codes = (v * np.exp2(127.0 - byte)[:, None, :]).reshape(n, m).astype(np.float32).astype(ml_dtypes.float8_e4m3fn).view(np.uint8)
    words = codes.reshape(n // 512, 128, 4, m).transpose(0, 1, 3, 2)
    return np.ascontiguousarray(words), np.ascontiguousarray(byte.astype(np.uint8).reshape(n // 512, 16, m))


K, T, S, H, W = 512, 2048, 512, 512, 256


def setup_inputs():
    n = np.random.standard_normal
    s = mx_kscale(K)[:, None]
    u = mx_kscale(S)
    packed_xT = pack_weight(n((K, T)) * s)
    perm = np.random.permutation(H)
    return {
        "x_words": packed_xT[0],
        "x_scales": packed_xT[1],
        "wa": (n((K, H)) / np.sqrt(K) / s).astype(np.float32),
        "wb": (n((K, H)) / np.sqrt(K) / s).astype(np.float32),
        "gt": (np.random.uniform(0.5, 1.5, (S, 1)) * u[:, None]).astype(np.float32),
        "gi": (np.random.uniform(0.5, 1.5, (S, 1)) / u[:, None]).astype(np.float32),
        "offs": striped(np.random.permutation(T)[:S]),
        "two": striped(np.random.permutation(T)[:S]),
        "n1": striped(np.random.permutation(H)),
        "n2": striped(np.random.permutation(H)),
        "n3": striped(perm[:W]),
        "n4": striped(perm[W:]),
    }


def reference(x_words, x_scales, wa, wb, gt, gi, offs, two, n1, n2, n3, n4):
    xq = unpack_weight(x_words, x_scales)[:, unstriped(offs)]
    a = xq.T @ mxq(f64(wa), 0, "e4m3")
    x_two = unpack_weight(x_words, x_scales)[:, unstriped(two)]
    b = x_two.T @ mxq(f64(wb), 0, "e4m3")
    z = f64(gt) * (a * (sigmoid(b[:, unstriped(n2)])) - (0.5 * a[:, unstriped(n1)]))
    z2 = f64(gi) * b
    cv = 0.0625 * ((mxq(z, 0, "e4m3").T @ mxq(z2, 0, "e4m3")))
    pa = cv[:, unstriped(n3)]
    pb = cv[:, unstriped(n4)]
    ra = pa * sigmoid(pb)
    out = cv.copy()
    out[:, unstriped(n4)] = ra
    return (out,) + planes(out)

@@ -1,0 +1,216 @@
+from contextlib import ExitStack
+
+import concourse.mybir as mybir
+
+K, T, S, H, W = 512, 2048, 512, 512, 256
+FLOPS = 3 * 2 * 512 * 512 * 512
+
+F32 = mybir.dt.float32
+BF16 = mybir.dt.bfloat16
+I32 = mybir.dt.int32
+U32 = mybir.dt.uint32
+U16 = mybir.dt.uint16
+U8 = mybir.dt.uint8
+FP8X4 = mybir.dt.float8_e4m3fn_x4
+ALU = mybir.AluOpType
+ACT = mybir.ActivationFunctionType
+
+P = 128
+PACK = 4
+HALF = 256
+LIST_COLS = HALF // 16
+
+
+def tile_picked_momtgatebfold_none_po_kernel(tc, x_words, x_scales, wa, wb, gt, gi, offs, two, n1, n2, n3, n4, out_0, out_1, out_2):
+    nc = tc.nc
+    with ExitStack() as ctx:
+        keep = ctx.enter_context(tc.tile_pool(name="keep", bufs=1))
+        psum = ctx.enter_context(tc.psum_pool(name="psum", bufs=1))
+
+        def sb(name, shape, dtype):
+            return keep.tile(shape, dtype, name=name, align_bytes=64)
+
+        def load_list(name, src):
+            tile = keep.tile(list(src.shape), U16, name=name)
+            nc.sync.dma_start(tile[:], src)
+            return tile
+
+        def load_weight_half(name, w, h):
+            raw = sb(name, [P, PACK, HALF], F32)
+            nc.sync.dma_start(raw[:], w.rearrange("(p j) c -> p j c", j=PACK)[:, :, h * HALF:(h + 1) * HALF])
+            return raw
+
+        def round_weight_half(name, raw, copy):
+            grouped = sb(name, [P, HALF * PACK], BF16)
+            copy(grouped[:].rearrange("p (c i j) -> p c j i", i=4, j=PACK), raw[:].rearrange("p j (c i) -> p c j i", i=4))
+            return grouped
+
+        def quantize(name, grouped, width):
+            codes = sb(name + "_codes", [P, width], U32)
+            scales = sb(name + "_scales", [P, width], U8)
+            nc.vector.quantize_mx(out=codes[:].bitcast(FP8X4), scales=scales[:], in_=grouped)
+            return codes, scales
+
+        def mx(out, lhs, cols, rhs):
+            nc.tensor.matmul_mx(out=out, lhsT=lhs[0][:, cols].bitcast(FP8X4), lhsT_scale=lhs[1][:, cols],
+                                rhs=rhs[0][:].bitcast(FP8X4), rhs_scale=rhs[1][:], start=True, stop=True)
+
+        xw = sb("xw", [P, T], U32)
+        xs = sb("xs", [P, T], U8)
+        nc.gpsimd.memset(xs[:].bitcast(I32), 0)
+        two_l = load_list("two_l", two)
+        offs_l = load_list("offs_l", offs)
+        for q in range(4):
+            nc.sync.dma_start(xs[32 * q:32 * q + 4, :].bitcast(I32), x_scales[0, 4 * q:4 * q + 4, :].bitcast(I32))
+        nc.sync.dma_start(xw[:].bitcast(I32), x_words[0].rearrange("p c r -> p (c r)").bitcast(I32))
+        wb_raw = [load_weight_half("wb_raw%d" % h, wb, h) for h in range(2)]
+        n2_l = load_list("n2_l", n2)
+        wa_raw = [load_weight_half("wa_raw%d" % h, wa, h) for h in range(2)]
+        gt_sb = sb("gt_sb", [P, PACK], F32)
+        gi_sb = sb("gi_sb", [P, PACK], F32)
+        nc.sync.dma_start(gt_sb[:], gt.rearrange("(p t) o -> p (t o)", t=PACK))
+        nc.sync.dma_start(gi_sb[:], gi.rearrange("(p t) o -> p (t o)", t=PACK))
+        n1_l = load_list("n1_l", n1)
+        n3_l = load_list("n3_l", n3)
+        n4_l = load_list("n4_l", n4)
+
+        def gather(name, window, lst, dtype):
+            picked = sb(name, [P, S], dtype)
+            nc.vector.tensor_copy(picked[:].rearrange("p (t m) -> p m t", t=PACK), window[:].indirect(lst[:]))
+            return picked
+
+        xb_s = gather("xb_s", xs, two_l, U8)
+        xa_s = gather("xa_s", xs, offs_l, U8)
+        xb_w = gather("xb_w", xw, two_l, U32)
+        wb_g = [round_weight_half("wb_g%d" % h, wb_raw[h], nc.scalar.copy) for h in range(2)]
+        wb_q = [quantize("wb0", wb_g[0][:], HALF)]
+        xa_w = gather("xa_w", xw, offs_l, U32)
+        wb_q.append(quantize("wb1", wb_g[1][:], HALF))
+
+        banks = [psum.tile([P, H], F32, name="bank%d" % i) for i in range(2 * PACK)]
+        b_ps, a_ps = banks[:PACK], banks[PACK:]
+        for h in range(2):
+            for t in range(PACK):
+                mx(b_ps[t][:, h * HALF:(h + 1) * HALF], (xb_w, xb_s), slice(t * P, (t + 1) * P), wb_q[h])
+
+        b_sb = [sb("b_sb%d" % t, [P, H], F32) for t in range(PACK)]
+        a_sb = [sb("a_sb%d" % t, [P, H], F32) for t in range(PACK)]
+        sig = [sb("sig%d" % t, [P, H], F32) for t in range(PACK)]
+        prod = [sb("prod%d" % s, [P, 2, H], F32) for s in range(2)]
+        picked_a = [sb("picked_a%d" % s, [P, 2, H], F32) for s in range(2)]
+        z_pairs = sb("z_pairs", [P, 2, H, 2], BF16)
+        z2_pairs = sb("z2_pairs", [P, 2, H, 2], BF16)
+
+        def fetch(out, window, lst, func):
+            for h in range(out.shape[1] // HALF):
+                nc.scalar.activation(out[:, h * HALF:(h + 1) * HALF],
+                                     window[:].indirect(lst[:, h * LIST_COLS:(h + 1) * LIST_COLS]), func)
+
+        nc.vector.tensor_copy(b_sb[0][:], b_ps[0][:])
+        fetch(sig[0][:], b_sb[0], n2_l, ACT.Sigmoid)
+        wa_g = [round_weight_half("wa_g%d" % h, wa_raw[h], copy) for h, copy in enumerate((nc.scalar.copy, nc.vector.tensor_copy))]
+        nc.vector.tensor_copy(b_sb[1][:], b_ps[1][:])
+        wa_q = [quantize("wa0", wa_g[0][:], HALF)]
+        nc.vector.tensor_copy(b_sb[2][:], b_ps[2][:])
+        wa_q.append(quantize("wa1", wa_g[1][:], HALF))
+        for h in range(2):
+            for t in range(PACK):
+                mx(a_ps[t][:, h * HALF:(h + 1) * HALF], (xa_w, xa_s), slice(t * P, (t + 1) * P), wa_q[h])
+        nc.vector.tensor_copy(b_sb[3][:], b_ps[3][:])
+
+        half_gt = sb("half_gt", [P, PACK], F32)
+        nc.vector.tensor_scalar(half_gt[:], gt_sb[:], 0.5, None, ALU.mult)
+
+        def half_a(t):
+            if t in ():
+                nc.vector.tensor_scalar(a_sb[t][:], a_ps[t][:], half_gt[:, t:t + 1], None, ALU.mult)
+            else:
+                nc.scalar.activation(a_sb[t][:], a_ps[t][:], ACT.Copy, scale=half_gt[:, t:t + 1])
+
+        def z2_tile(t):
+            nc.vector.tensor_scalar(z2_pairs[:, t // 2, :, t % 2], b_sb[t][:], gi_sb[:, t:t + 1], None, ALU.mult)
+
+        def gated(t):
+            nc.vector.scalar_tensor_tensor(prod[t // 2][:, t % 2, :], a_ps[t][:], gt_sb[:, t:t + 1], sig[t][:], ALU.mult, ALU.mult)
+
+        def z_pair(s):
+            nc.vector.tensor_tensor(z_pairs[:, s].rearrange("p (u m) e -> p m u e", u=PACK),
+                                    prod[s][:].rearrange("p e (m u) -> p m u e", u=PACK),
+                                    picked_a[s][:].rearrange("p e (m u) -> p m u e", u=PACK), ALU.subtract)
+
+        def weave(out, pairs, cols):
+            words = pairs[:].rearrange("p s c e -> p s (c e)").bitcast(I32)
+            nc.vector.tensor_copy(out.bitcast(I32).rearrange("p (c s) -> p c s", s=2), words[:, :, cols].rearrange("p s c -> p c s"))
+
+        def fetch_gate(t):
+            fetch(sig[t][:], b_sb[t], n2_l, ACT.Sigmoid)
+
+        def fetch_a(t):
+            half_a(t)
+            fetch(picked_a[t // 2][:, t % 2, :], a_sb[t], n1_l, ACT.Copy)
+
+        fetch_gate(1)
+        fetch_a(0)
+        gated(0)
+        z2_tile(0)
+        fetch_a(1)
+        gated(1)
+        z2_tile(1)
+        fetch_gate(2)
+        z2_tile(2)
+        z2_tile(3)
+        z_pair(0)
+        fetch_gate(3)
+        z2_g = sb("z2_g", [P, H * PACK], BF16)
+        weave(z2_g[:], z2_pairs, slice(0, H))
+        gated(2)
+        z2_q = quantize("zb", z2_g[:], H)
+        fetch_a(2)
+        gated(3)
+        fetch_a(3)
+        z_pair(1)
+
+        z_g = [sb("z_g%d" % u, [P, P * PACK], BF16) for u in range(PACK)]
+        for u in range(PACK):
+            weave(z_g[u][:], z_pairs, slice(u * P, (u + 1) * P))
+        z_q = [quantize("za%d" % u, z_g[u][:], P) for u in range(PACK)]
+        for u in range(PACK):
+            mx(b_ps[u][:], z_q[u], slice(0, P), z2_q)
+
+        cv = [sb("cv%d" % u, [P, H], F32) for u in range(PACK)]
+        y = [sb("y%d" % u, [P, H], F32) for u in range(PACK)]
+        pa = [sb("pa%d" % u, [P, W], F32) for u in range(PACK)]
+        gate = [sb("gate%d" % u, [P, W], F32) for u in range(PACK)]
+        ra = [sb("ra%d" % u, [P, W], F32) for u in range(PACK)]
+        y_g = [sb("y_g%d" % h, [P, HALF, PACK], BF16) for h in range(2)]
+        out_rows = out_0.rearrange("(p u) c -> p u c", u=PACK)
+
+        def fold_fetch(u):
+            nc.vector.tensor_scalar(cv[u][:], b_ps[u][:], 0.0625, None, ALU.mult)
+            nc.scalar.activation(gate[u][:], cv[u][:].indirect(n4_l[:]), ACT.Sigmoid)
+            nc.scalar.activation(pa[u][:], cv[u][:].indirect(n3_l[:]), ACT.Copy)
+            nc.vector.tensor_copy(y[u][:], cv[u][:])
+            nc.vector.tensor_tensor(ra[u][:], pa[u][:], gate[u][:], ALU.mult)
+
+        def fold_put(u):
+            nc.scalar.activation(y[u][:].indirect(n4_l[:]), ra[u][:], ACT.Copy)
+            nc.sync.dma_start(out_rows[:, u, :], y[u][:])
+            for h in range(2):
+                nc.vector.tensor_copy(y_g[h][:, :, u], y[u][:, h * HALF:(h + 1) * HALF])
+
+        fold_fetch(0)
+        for u in range(1, PACK):
+            fold_fetch(u)
+            fold_put(u - 1)
+        fold_put(PACK - 1)
+
+        y_codes = sb("y_codes", [P, H], U32)
+        y_scales = sb("y_scales", [P, H], U8)
+        out_words = out_1[0].rearrange("p c r -> p (c r)").bitcast(I32)
+        for h in range(2):
+            cols = slice(h * HALF, (h + 1) * HALF)
+            nc.vector.quantize_mx(out=y_codes[:, cols].bitcast(FP8X4), scales=y_scales[:, cols],
+                                  in_=y_g[h][:].rearrange("p c u -> p (c u)"))
+            nc.sync.dma_start(out_words[:, cols], y_codes[:, cols].bitcast(I32))
+        for q in range(4):
+            nc.scalar.dma_start(out_2[0, 4 * q:4 * q + 4, :].bitcast(I32), y_scales[32 * q:32 * q + 4, :].bitcast(I32))

@@ -18,7 +18,7 @@ ACT = mybir.ActivationFunctionType
 P = 128
 PACK = 4
 HALF = 256
-LIST_COLS = HALF // 16
+QUARTER = 128
 
 
 def tile_picked_momtgatebfold_none_po_kernel(tc, x_words, x_scales, wa, wb, gt, gi, offs, two, n1, n2, n3, n4, out_0, out_1, out_2):
@@ -27,8 +27,8 @@ def tile_picked_momtgatebfold_none_po_kernel(tc, x_words, x_scales, wa, wb, gt, 
         keep = ctx.enter_context(tc.tile_pool(name="keep", bufs=1))
         psum = ctx.enter_context(tc.psum_pool(name="psum", bufs=1))
 
-        def sb(name, shape, dtype):
-            return keep.tile(shape, dtype, name=name, align_bytes=64)
+        def sb(name, shape, dtype, tag=None):
+            return keep.tile(shape, dtype, name=name, tag=tag or name, align_bytes=64)
 
         def load_list(name, src):
             tile = keep.tile(list(src.shape), U16, name=name)
@@ -40,39 +40,54 @@ def tile_picked_momtgatebfold_none_po_kernel(tc, x_words, x_scales, wa, wb, gt, 
             nc.sync.dma_start(raw[:], w.rearrange("(p j) c -> p j c", j=PACK)[:, :, h * HALF:(h + 1) * HALF])
             return raw
 
-        def round_weight_half(name, raw, copy):
+        def round_on_scalar(name, raw):
             grouped = sb(name, [P, HALF * PACK], BF16)
-            copy(grouped[:].rearrange("p (c i j) -> p c j i", i=4, j=PACK), raw[:].rearrange("p j (c i) -> p c j i", i=4))
+            nc.scalar.copy(grouped[:].rearrange("p (c i j) -> p c j i", i=4, j=PACK), raw[:].rearrange("p j (c i) -> p c j i", i=4))
+            return grouped
+
+        def round_on_gpsimd(name, raw):
+            grouped = sb(name, [P, HALF * PACK], BF16)
+            nc.gpsimd.tensor_scalar(grouped[:].rearrange("p (c j) -> p c j", j=PACK), raw[:].rearrange("p j c -> p c j"),
+                                    1.0, 0.0, ALU.mult, ALU.add)
             return grouped
 
         def quantize(name, grouped, width):
             codes = sb(name + "_codes", [P, width], U32)
             scales = sb(name + "_scales", [P, width], U8)
-            nc.vector.quantize_mx(out=codes[:].bitcast(FP8X4), scales=scales[:], in_=grouped)
+            nc.vector.quantize_mx(out=codes[:].bitcast(FP8X4), scales=scales[:], in_=grouped[:])
             return codes, scales
 
-        def mx(out, lhs, cols, rhs):
-            nc.tensor.matmul_mx(out=out, lhsT=lhs[0][:, cols].bitcast(FP8X4), lhsT_scale=lhs[1][:, cols],
-                                rhs=rhs[0][:].bitcast(FP8X4), rhs_scale=rhs[1][:], start=True, stop=True)
+        def quantize_half(planes, h, grouped):
+            cols = slice(h * HALF, (h + 1) * HALF)
+            nc.vector.quantize_mx(out=planes[0][:, cols].bitcast(FP8X4), scales=planes[1][:, cols], in_=grouped)
+
+        def mx(out, lhs, lhs_cols, rhs, rhs_cols):
+            nc.tensor.matmul_mx(out=out, lhsT=lhs[0][:, lhs_cols].bitcast(FP8X4), lhsT_scale=lhs[1][:, lhs_cols],
+                                rhs=rhs[0][:, rhs_cols].bitcast(FP8X4), rhs_scale=rhs[1][:, rhs_cols], start=True, stop=True)
 
         xw = sb("xw", [P, T], U32)
         xs = sb("xs", [P, T], U8)
-        nc.gpsimd.memset(xs[:].bitcast(I32), 0)
+        nc.vector.memset(xs[:].bitcast(I32), 0)
         two_l = load_list("two_l", two)
         offs_l = load_list("offs_l", offs)
+        wb_raw = [load_weight_half("wb_raw0", wb, 0)]
         for q in range(4):
             nc.sync.dma_start(xs[32 * q:32 * q + 4, :].bitcast(I32), x_scales[0, 4 * q:4 * q + 4, :].bitcast(I32))
+        wb_raw.append(load_weight_half("wb_raw1", wb, 1))
         nc.sync.dma_start(xw[:].bitcast(I32), x_words[0].rearrange("p c r -> p (c r)").bitcast(I32))
-        wb_raw = [load_weight_half("wb_raw%d" % h, wb, h) for h in range(2)]
         n2_l = load_list("n2_l", n2)
         wa_raw = [load_weight_half("wa_raw%d" % h, wa, h) for h in range(2)]
         gt_sb = sb("gt_sb", [P, PACK], F32)
         gi_sb = sb("gi_sb", [P, PACK], F32)
-        nc.sync.dma_start(gt_sb[:], gt.rearrange("(p t) o -> p (t o)", t=PACK))
         nc.sync.dma_start(gi_sb[:], gi.rearrange("(p t) o -> p (t o)", t=PACK))
+        nc.sync.dma_start(gt_sb[:], gt.rearrange("(p t) o -> p (t o)", t=PACK))
         n1_l = load_list("n1_l", n1)
-        n3_l = load_list("n3_l", n3)
         n4_l = load_list("n4_l", n4)
+        n3_l = load_list("n3_l", n3)
+
+        warm = sb("warm", [P, 2], F32)
+        nc.vector.memset(warm[:, 0:1], 0.0)
+        nc.scalar.activation(warm[:, 1:2], warm[:, 0:1], ACT.Sigmoid)
 
         def gather(name, window, lst, dtype):
             picked = sb(name, [P, S], dtype)
@@ -81,101 +96,87 @@ def tile_picked_momtgatebfold_none_po_kernel(tc, x_words, x_scales, wa, wb, gt, 
 
         xb_s = gather("xb_s", xs, two_l, U8)
         xa_s = gather("xa_s", xs, offs_l, U8)
+        wb_q = (sb("wb_codes", [P, H], U32, "xs"), sb("wb_scales", [P, H], U8))
+        wa_q = (sb("wa_codes", [P, H], U32), sb("wa_scales", [P, H], U8))
+        for h in range(2):
+            quantize_half(wb_q, h, round_on_scalar("wb_g%d" % h, wb_raw[h])[:])
         xb_w = gather("xb_w", xw, two_l, U32)
-        wb_g = [round_weight_half("wb_g%d" % h, wb_raw[h], nc.scalar.copy) for h in range(2)]
-        wb_q = [quantize("wb0", wb_g[0][:], HALF)]
         xa_w = gather("xa_w", xw, offs_l, U32)
-        wb_q.append(quantize("wb1", wb_g[1][:], HALF))
+        wa_g = [round_on_scalar("wa_g0", wa_raw[0]), round_on_gpsimd("wa_g1", wa_raw[1])]
 
         banks = [psum.tile([P, H], F32, name="bank%d" % i) for i in range(2 * PACK)]
         b_ps, a_ps = banks[:PACK], banks[PACK:]
-        for h in range(2):
-            for t in range(PACK):
-                mx(b_ps[t][:, h * HALF:(h + 1) * HALF], (xb_w, xb_s), slice(t * P, (t + 1) * P), wb_q[h])
 
-        b_sb = [sb("b_sb%d" % t, [P, H], F32) for t in range(PACK)]
-        a_sb = [sb("a_sb%d" % t, [P, H], F32) for t in range(PACK)]
+        def project(ps, picked, w_q):
+            for t in range(PACK):
+                mx(ps[t][:], picked, slice(t * P, (t + 1) * P), w_q, slice(0, H))
+
+        b_sb = []
+        a_sb = [sb("a_sb%d" % t, [P, H + 16], F32) for t in range(PACK)]
         sig = [sb("sig%d" % t, [P, H], F32) for t in range(PACK)]
         prod = [sb("prod%d" % s, [P, 2, H], F32) for s in range(2)]
         picked_a = [sb("picked_a%d" % s, [P, 2, H], F32) for s in range(2)]
         z_pairs = sb("z_pairs", [P, 2, H, 2], BF16)
         z2_pairs = sb("z2_pairs", [P, 2, H, 2], BF16)
 
-        def fetch(out, window, lst, func):
-            for h in range(out.shape[1] // HALF):
-                nc.scalar.activation(out[:, h * HALF:(h + 1) * HALF],
-                                     window[:].indirect(lst[:, h * LIST_COLS:(h + 1) * LIST_COLS]), func)
+        def fetch(out, window, lst, func, lo, hi):
+            nc.scalar.activation(out[:, lo:hi], window[:].indirect(lst[:, lo // 16:hi // 16]), func)
 
-        nc.vector.tensor_copy(b_sb[0][:], b_ps[0][:])
-        fetch(sig[0][:], b_sb[0], n2_l, ACT.Sigmoid)
-        wa_g = [round_weight_half("wa_g%d" % h, wa_raw[h], copy) for h, copy in enumerate((nc.scalar.copy, nc.vector.tensor_copy))]
-        nc.vector.tensor_copy(b_sb[1][:], b_ps[1][:])
-        wa_q = [quantize("wa0", wa_g[0][:], HALF)]
-        nc.vector.tensor_copy(b_sb[2][:], b_ps[2][:])
-        wa_q.append(quantize("wa1", wa_g[1][:], HALF))
-        for h in range(2):
-            for t in range(PACK):
-                mx(a_ps[t][:, h * HALF:(h + 1) * HALF], (xa_w, xa_s), slice(t * P, (t + 1) * P), wa_q[h])
-        nc.vector.tensor_copy(b_sb[3][:], b_ps[3][:])
-
-        half_gt = sb("half_gt", [P, PACK], F32)
-        nc.vector.tensor_scalar(half_gt[:], gt_sb[:], 0.5, None, ALU.mult)
+        def fetch_gate(t, copy, tag=None):
+            b_sb.append(sb("b_sb%d" % t, [P, 2 * H], F32, tag))
+            copy(b_sb[t][:, :H], b_ps[t][:])
+            fetch(sig[t][:], b_sb[t], n2_l, ACT.Sigmoid, 0, H)
+            nc.gpsimd.tensor_scalar(z2_pairs[:, t // 2, :, t % 2], b_sb[t][:, :H], gi_sb[:, t:t + 1], 0.0, ALU.mult, ALU.add)
 
         def half_a(t):
-            if t in ():
-                nc.vector.tensor_scalar(a_sb[t][:], a_ps[t][:], half_gt[:, t:t + 1], None, ALU.mult)
-            else:
-                nc.scalar.activation(a_sb[t][:], a_ps[t][:], ACT.Copy, scale=half_gt[:, t:t + 1])
+            nc.vector.tensor_scalar(a_sb[t][:, :H], a_ps[t][:], gt_sb[:, t:t + 1], 0.5, ALU.mult, ALU.mult)
 
-        def z2_tile(t):
-            nc.vector.tensor_scalar(z2_pairs[:, t // 2, :, t % 2], b_sb[t][:], gi_sb[:, t:t + 1], None, ALU.mult)
+        def fetch_a(t, lo, hi):
+            fetch(picked_a[t // 2][:, t % 2, :], a_sb[t], n1_l, ACT.Copy, lo, hi)
 
         def gated(t):
             nc.vector.scalar_tensor_tensor(prod[t // 2][:, t % 2, :], a_ps[t][:], gt_sb[:, t:t + 1], sig[t][:], ALU.mult, ALU.mult)
 
-        def z_pair(s):
-            nc.vector.tensor_tensor(z_pairs[:, s].rearrange("p (u m) e -> p m u e", u=PACK),
-                                    prod[s][:].rearrange("p e (m u) -> p m u e", u=PACK),
-                                    picked_a[s][:].rearrange("p e (m u) -> p m u e", u=PACK), ALU.subtract)
+        def z_pair(s, lo, hi):
+            rows = slice(lo // PACK, hi // PACK)
+            nc.vector.tensor_tensor(z_pairs[:, s].rearrange("p (u m) e -> p m u e", u=PACK)[:, rows],
+                                    prod[s][:].rearrange("p e (m u) -> p m u e", u=PACK)[:, rows],
+                                    picked_a[s][:].rearrange("p e (m u) -> p m u e", u=PACK)[:, rows], ALU.subtract)
 
-        def weave(out, pairs, cols):
+        def z_single(t, lo, hi):
+            rows = slice(lo // PACK, hi // PACK)
+            nc.vector.tensor_tensor(z_pairs[:, t // 2, :, t % 2].rearrange("p (u m) -> p m u", u=PACK)[:, rows],
+                                    prod[t // 2][:, t % 2, :].rearrange("p (m u) -> p m u", u=PACK)[:, rows],
+                                    picked_a[t // 2][:, t % 2, :].rearrange("p (m u) -> p m u", u=PACK)[:, rows], ALU.subtract)
+
+        def weave(name, pairs, lo, hi, engine=nc.vector):
+            grouped = sb(name, [P, (hi - lo) * PACK], BF16)
             words = pairs[:].rearrange("p s c e -> p s (c e)").bitcast(I32)
-            nc.vector.tensor_copy(out.bitcast(I32).rearrange("p (c s) -> p c s", s=2), words[:, :, cols].rearrange("p s c -> p c s"))
+            engine.tensor_copy(grouped[:].bitcast(I32).rearrange("p (c s) -> p c s", s=2),
+                                  words[:, :, lo:hi].rearrange("p s c -> p c s"))
+            return grouped
 
-        def fetch_gate(t):
-            fetch(sig[t][:], b_sb[t], n2_l, ACT.Sigmoid)
-
-        def fetch_a(t):
-            half_a(t)
-            fetch(picked_a[t // 2][:, t % 2, :], a_sb[t], n1_l, ACT.Copy)
-
-        fetch_gate(1)
-        fetch_a(0)
-        gated(0)
-        z2_tile(0)
-        fetch_a(1)
-        gated(1)
-        z2_tile(1)
-        fetch_gate(2)
-        z2_tile(2)
-        z2_tile(3)
-        z_pair(0)
-        fetch_gate(3)
-        z2_g = sb("z2_g", [P, H * PACK], BF16)
-        weave(z2_g[:], z2_pairs, slice(0, H))
-        gated(2)
-        z2_q = quantize("zb", z2_g[:], H)
-        fetch_a(2)
-        gated(3)
-        fetch_a(3)
-        z_pair(1)
-
-        z_g = [sb("z_g%d" % u, [P, P * PACK], BF16) for u in range(PACK)]
-        for u in range(PACK):
-            weave(z_g[u][:], z_pairs, slice(u * P, (u + 1) * P))
-        z_q = [quantize("za%d" % u, z_g[u][:], P) for u in range(PACK)]
-        for u in range(PACK):
-            mx(b_ps[u][:], z_q[u], slice(0, P), z2_q)
+        project(b_ps, (xb_w, xb_s), wb_q)
+        fetch_gate(0, nc.scalar.copy, "wa_raw0")
+        fetch_gate(1, nc.vector.tensor_copy)
+        quantize_half(wa_q, 0, wa_g[0][:])
+        fetch_gate(2, nc.vector.tensor_copy)
+        quantize_half(wa_q, 1, wa_g[1][:])
+        project(a_ps, (xa_w, xa_s), wa_q)
+        fetch_gate(3, nc.vector.tensor_copy, "wa_g1")
+        for s in range(2):
+            for t in (2 * s, 2 * s + 1):
+                half_a(t)
+            for t in (2 * s, 2 * s + 1):
+                gated(t)
+        z2_q = quantize("zb", weave("z2_g", z2_pairs, 0, H, nc.gpsimd), H)
+        for t in (0, 1):
+            fetch_a(t, 0, H)
+        z_pair(0, 0, H)
+        for t, cuts in ((2, (0, H)), (3, (0, H - QUARTER, H))):
+            for lo, hi in zip(cuts, cuts[1:]):
+                fetch_a(t, lo, hi)
+                z_single(t, lo, hi)
 
         cv = [sb("cv%d" % u, [P, H], F32) for u in range(PACK)]
         y = [sb("y%d" % u, [P, H], F32) for u in range(PACK)]
@@ -185,24 +186,27 @@ def tile_picked_momtgatebfold_none_po_kernel(tc, x_words, x_scales, wa, wb, gt, 
         y_g = [sb("y_g%d" % h, [P, HALF, PACK], BF16) for h in range(2)]
         out_rows = out_0.rearrange("(p u) c -> p u c", u=PACK)
 
-        def fold_fetch(u):
+        z_g = [weave("z_g%d" % u, z_pairs, u * P, (u + 1) * P) for u in range(2)]
+        z_q = quantize("za0", z_g[0], P)
+        mx(b_ps[0][:, :HALF], z_q, slice(0, P), z2_q, slice(0, HALF))
+        mx(a_ps[0][:, :HALF], z_q, slice(0, P), z2_q, slice(HALF, H))
+        nc.scalar.activation(cv[0][:, :HALF], b_ps[0][:, :HALF], ACT.Copy, scale=0.0625)
+        nc.scalar.activation(cv[0][:, HALF:], a_ps[0][:, :HALF], ACT.Copy, scale=0.0625)
+        for u in range(1, PACK):
+            if u + 1 < PACK:
+                z_g.append(weave("z_g%d" % (u + 1), z_pairs, (u + 1) * P, (u + 2) * P))
+            mx(b_ps[u][:], quantize("za%d" % u, z_g[u], P), slice(0, P), z2_q, slice(0, H))
             nc.vector.tensor_scalar(cv[u][:], b_ps[u][:], 0.0625, None, ALU.mult)
+        for u in range(PACK):
             nc.scalar.activation(gate[u][:], cv[u][:].indirect(n4_l[:]), ACT.Sigmoid)
             nc.scalar.activation(pa[u][:], cv[u][:].indirect(n3_l[:]), ACT.Copy)
             nc.vector.tensor_copy(y[u][:], cv[u][:])
             nc.vector.tensor_tensor(ra[u][:], pa[u][:], gate[u][:], ALU.mult)
-
-        def fold_put(u):
+        for u in range(PACK):
             nc.scalar.activation(y[u][:].indirect(n4_l[:]), ra[u][:], ACT.Copy)
             nc.sync.dma_start(out_rows[:, u, :], y[u][:])
             for h in range(2):
                 nc.vector.tensor_copy(y_g[h][:, :, u], y[u][:, h * HALF:(h + 1) * HALF])
-
-        fold_fetch(0)
-        for u in range(1, PACK):
-            fold_fetch(u)
-            fold_put(u - 1)
-        fold_put(PACK - 1)
 
         y_codes = sb("y_codes", [P, H], U32)
         y_scales = sb("y_scales", [P, H], U8)
@@ -213,4 +217,4 @@ def tile_picked_momtgatebfold_none_po_kernel(tc, x_words, x_scales, wa, wb, gt, 
                                   in_=y_g[h][:].rearrange("p c u -> p (c u)"))
             nc.sync.dma_start(out_words[:, cols], y_codes[:, cols].bitcast(I32))
         for q in range(4):
-            nc.scalar.dma_start(out_2[0, 4 * q:4 * q + 4, :].bitcast(I32), y_scales[32 * q:32 * q + 4, :].bitcast(I32))
+            (nc.scalar, nc.sync)[q % 2].dma_start(out_2[0, 4 * q:4 * q + 4, :].bitcast(I32), y_scales[32 * q:32 * q + 4, :].bitcast(I32))

@@ -2,7 +2,7 @@ from contextlib import ExitStack
 
 import concourse.mybir as mybir
 
-K, T, S, H, W = 512, 2048, 512, 512, 256
+T, S, H, W = 2048, 512, 512, 256
 FLOPS = 3 * 2 * 512 * 512 * 512
 
 F32 = mybir.dt.float32
@@ -17,66 +17,65 @@ ACT = mybir.ActivationFunctionType
 
 P = 128
 PACK = 4
-HALF = 256
-QUARTER = 128
+QUADRANTS = 4
+HALF = H // 2
+QUARTER = H // 4
+LIST_ROWS = 16
+WA_PIECES = ((0, QUARTER), (QUARTER, HALF), (HALF, H))
+A_WINDOW = H + 16
+B_WINDOW = 2 * H
+CV_SCALE = 0.0625
 
 
-def tile_picked_momtgatebfold_none_po_kernel(tc, x_words, x_scales, wa, wb, gt, gi, offs, two, n1, n2, n3, n4, out_0, out_1, out_2):
+def tile_picked_momtgatebfold_none_po_kernel(
+        tc, x_words, x_scales, wa, wb, gt, gi, offs, two, n1, n2, n3, n4, out_0, out_1, out_2):
     nc = tc.nc
     with ExitStack() as ctx:
         keep = ctx.enter_context(tc.tile_pool(name="keep", bufs=1))
         psum = ctx.enter_context(tc.psum_pool(name="psum", bufs=1))
 
-        def sb(name, shape, dtype, tag=None):
-            return keep.tile(shape, dtype, name=name, tag=tag or name, align_bytes=64)
+        def sb(name, shape, dtype, after=None):
+            return keep.tile(shape, dtype, name=name, tag=after or name, align_bytes=64)
 
         def load_list(name, src):
             tile = keep.tile(list(src.shape), U16, name=name)
             nc.sync.dma_start(tile[:], src)
             return tile
 
-        def load_weight_half(name, w, h):
-            raw = sb(name, [P, PACK, HALF], F32)
-            nc.sync.dma_start(raw[:], w.rearrange("(p j) c -> p j c", j=PACK)[:, :, h * HALF:(h + 1) * HALF])
+        def load_columns(name, w, lo, hi):
+            raw = sb(name, [P, PACK, hi - lo], F32)
+            nc.sync.dma_start(raw[:], w.rearrange("(p j) c -> p j c", j=PACK)[:, :, lo:hi])
             return raw
 
-        def round_on_scalar(name, raw):
-            grouped = sb(name, [P, HALF * PACK], BF16)
-            nc.scalar.copy(grouped[:].rearrange("p (c i j) -> p c j i", i=4, j=PACK), raw[:].rearrange("p j (c i) -> p c j i", i=4))
-            return grouped
+        def round_weights(copy, grouped, raw):
+            copy(grouped.rearrange("p (c i j) -> p c j i", i=4, j=PACK), raw[:].rearrange("p j (c i) -> p c j i", i=4))
 
-        def round_on_gpsimd(name, raw):
-            grouped = sb(name, [P, HALF * PACK], BF16)
-            nc.gpsimd.tensor_scalar(grouped[:].rearrange("p (c j) -> p c j", j=PACK), raw[:].rearrange("p j c -> p c j"),
-                                    1.0, 0.0, ALU.mult, ALU.add)
-            return grouped
+        def planes(name, width, after=None):
+            return sb(name + "_codes", [P, width], U32, after), sb(name + "_scales", [P, width], U8)
 
-        def quantize(name, grouped, width):
-            codes = sb(name + "_codes", [P, width], U32)
-            scales = sb(name + "_scales", [P, width], U8)
-            nc.vector.quantize_mx(out=codes[:].bitcast(FP8X4), scales=scales[:], in_=grouped[:])
-            return codes, scales
-
-        def quantize_half(planes, h, grouped):
-            cols = slice(h * HALF, (h + 1) * HALF)
-            nc.vector.quantize_mx(out=planes[0][:, cols].bitcast(FP8X4), scales=planes[1][:, cols], in_=grouped)
+        def quantize(operand, cols, grouped):
+            nc.vector.quantize_mx(out=operand[0][:, cols].bitcast(FP8X4), scales=operand[1][:, cols], in_=grouped)
 
         def mx(out, lhs, lhs_cols, rhs, rhs_cols):
             nc.tensor.matmul_mx(out=out, lhsT=lhs[0][:, lhs_cols].bitcast(FP8X4), lhsT_scale=lhs[1][:, lhs_cols],
                                 rhs=rhs[0][:, rhs_cols].bitcast(FP8X4), rhs_scale=rhs[1][:, rhs_cols], start=True, stop=True)
 
-        xw = sb("xw", [P, T], U32)
-        xs = sb("xs", [P, T], U8)
-        nc.vector.memset(xs[:].bitcast(I32), 0)
+        halves = [slice(0, HALF), slice(HALF, H)]
+        row_tiles = [slice(t * P, (t + 1) * P) for t in range(PACK)]
+        all_cols = slice(0, H)
+
+        x_codes = sb("x_codes", [P, T], U32)
+        x_bytes = sb("x_bytes", [P, T], U8)
+        nc.vector.memset(x_bytes[:].bitcast(I32), 0)
         two_l = load_list("two_l", two)
         offs_l = load_list("offs_l", offs)
-        wb_raw = [load_weight_half("wb_raw0", wb, 0)]
-        for q in range(4):
-            nc.sync.dma_start(xs[32 * q:32 * q + 4, :].bitcast(I32), x_scales[0, 4 * q:4 * q + 4, :].bitcast(I32))
-        wb_raw.append(load_weight_half("wb_raw1", wb, 1))
-        nc.sync.dma_start(xw[:].bitcast(I32), x_words[0].rearrange("p c r -> p (c r)").bitcast(I32))
+        wb_raw = [load_columns("wb_raw0", wb, 0, HALF)]
+        for q in range(QUADRANTS):
+            nc.sync.dma_start(x_bytes[32 * q:32 * q + 4, :].bitcast(I32), x_scales[0, 4 * q:4 * q + 4, :].bitcast(I32))
+        wb_raw.append(load_columns("wb_raw1", wb, HALF, H))
+        nc.sync.dma_start(x_codes[:].bitcast(I32), x_words[0].rearrange("p c r -> p (c r)").bitcast(I32))
         n2_l = load_list("n2_l", n2)
-        wa_raw = [load_weight_half("wa_raw%d" % h, wa, h) for h in range(2)]
+        wa_raw = [load_columns("wa_raw%d" % i, wa, lo, hi) for i, (lo, hi) in enumerate(WA_PIECES)]
         gt_sb = sb("gt_sb", [P, PACK], F32)
         gi_sb = sb("gi_sb", [P, PACK], F32)
         nc.sync.dma_start(gi_sb[:], gi.rearrange("(p t) o -> p (t o)", t=PACK))
@@ -89,132 +88,128 @@ def tile_picked_momtgatebfold_none_po_kernel(tc, x_words, x_scales, wa, wb, gt, 
         nc.vector.memset(warm[:, 0:1], 0.0)
         nc.scalar.activation(warm[:, 1:2], warm[:, 0:1], ACT.Sigmoid)
 
-        def gather(name, window, lst, dtype):
+        def pick(name, window, entries, dtype):
             picked = sb(name, [P, S], dtype)
-            nc.vector.tensor_copy(picked[:].rearrange("p (t m) -> p m t", t=PACK), window[:].indirect(lst[:]))
+            nc.vector.tensor_copy(picked[:].rearrange("p (t m) -> p m t", t=PACK), window[:].indirect(entries[:]))
             return picked
 
-        xb_s = gather("xb_s", xs, two_l, U8)
-        xa_s = gather("xa_s", xs, offs_l, U8)
-        wb_q = (sb("wb_codes", [P, H], U32, "xs"), sb("wb_scales", [P, H], U8))
-        wa_q = (sb("wa_codes", [P, H], U32), sb("wa_scales", [P, H], U8))
+        xb_bytes = pick("xb_bytes", x_bytes, two_l, U8)
+        xa_bytes = pick("xa_bytes", x_bytes, offs_l, U8)
+        wb_q = planes("wb", H, after="x_bytes")
         for h in range(2):
-            quantize_half(wb_q, h, round_on_scalar("wb_g%d" % h, wb_raw[h])[:])
-        xb_w = gather("xb_w", xw, two_l, U32)
-        xa_w = gather("xa_w", xw, offs_l, U32)
-        wa_g = [round_on_scalar("wa_g0", wa_raw[0]), round_on_gpsimd("wa_g1", wa_raw[1])]
+            wb_g = sb("wb_g%d" % h, [P, HALF * PACK], BF16)
+            round_weights(nc.scalar.copy, wb_g[:], wb_raw[h])
+            quantize(wb_q, halves[h], wb_g[:])
+        xb_q = (pick("xb_codes", x_codes, two_l, U32), xb_bytes)
+        xa_q = (pick("xa_codes", x_codes, offs_l, U32), xa_bytes)
+        wa_q = planes("wa", H)
+        wa_g = [sb("wa_g%d" % h, [P, HALF * PACK], BF16) for h in range(2)]
+        round_weights(nc.scalar.copy, wa_g[0][:, :QUARTER * PACK], wa_raw[0])
+        round_weights(nc.vector.tensor_copy, wa_g[0][:, QUARTER * PACK:], wa_raw[1])
+        nc.gpsimd.tensor_scalar(wa_g[1][:].rearrange("p (c j) -> p c j", j=PACK), wa_raw[2][:].rearrange("p j c -> p c j"),
+                                1.0, 0.0, ALU.mult, ALU.add)
 
         banks = [psum.tile([P, H], F32, name="bank%d" % i) for i in range(2 * PACK)]
-        b_ps, a_ps = banks[:PACK], banks[PACK:]
-
-        def project(ps, picked, w_q):
-            for t in range(PACK):
-                mx(ps[t][:], picked, slice(t * P, (t + 1) * P), w_q, slice(0, H))
+        a_ps = banks[PACK:]
 
         b_sb = []
-        a_sb = [sb("a_sb%d" % t, [P, H + 16], F32) for t in range(PACK)]
-        sig = [sb("sig%d" % t, [P, H], F32) for t in range(PACK)]
-        prod = [sb("prod%d" % s, [P, 2, H], F32) for s in range(2)]
+        half_a = [sb("half_a%d" % t, [P, A_WINDOW], F32) for t in range(PACK)]
+        b_gate = [sb("b_gate%d" % t, [P, H], F32) for t in range(PACK)]
+        gated_a = [sb("gated_a%d" % s, [P, 2, H], F32) for s in range(2)]
         picked_a = [sb("picked_a%d" % s, [P, 2, H], F32) for s in range(2)]
         z_pairs = sb("z_pairs", [P, 2, H, 2], BF16)
         z2_pairs = sb("z2_pairs", [P, 2, H, 2], BF16)
 
-        def fetch(out, window, lst, func, lo, hi):
-            nc.scalar.activation(out[:, lo:hi], window[:].indirect(lst[:, lo // 16:hi // 16]), func)
-
-        def fetch_gate(t, copy, tag=None):
-            b_sb.append(sb("b_sb%d" % t, [P, 2 * H], F32, tag))
-            copy(b_sb[t][:, :H], b_ps[t][:])
-            fetch(sig[t][:], b_sb[t], n2_l, ACT.Sigmoid, 0, H)
+        def b_tile(t, copy, after=None):
+            b_sb.append(sb("b_sb%d" % t, [P, B_WINDOW], F32, after))
+            mx(banks[t % 2][:], xb_q, row_tiles[t], wb_q, all_cols)
+            copy(b_sb[t][:, :H], banks[t % 2][:])
+            nc.scalar.activation(b_gate[t][:], b_sb[t][:].indirect(n2_l[:]), ACT.Sigmoid)
             nc.gpsimd.tensor_scalar(z2_pairs[:, t // 2, :, t % 2], b_sb[t][:, :H], gi_sb[:, t:t + 1], 0.0, ALU.mult, ALU.add)
 
-        def half_a(t):
-            nc.vector.tensor_scalar(a_sb[t][:, :H], a_ps[t][:], gt_sb[:, t:t + 1], 0.5, ALU.mult, ALU.mult)
-
         def fetch_a(t, lo, hi):
-            fetch(picked_a[t // 2][:, t % 2, :], a_sb[t], n1_l, ACT.Copy, lo, hi)
-
-        def gated(t):
-            nc.vector.scalar_tensor_tensor(prod[t // 2][:, t % 2, :], a_ps[t][:], gt_sb[:, t:t + 1], sig[t][:], ALU.mult, ALU.mult)
+            nc.scalar.activation(picked_a[t // 2][:, t % 2, lo:hi],
+                                 half_a[t][:].indirect(n1_l[:, lo // LIST_ROWS:hi // LIST_ROWS]), ACT.Copy)
 
         def z_pair(s, lo, hi):
-            rows = slice(lo // PACK, hi // PACK)
-            nc.vector.tensor_tensor(z_pairs[:, s].rearrange("p (u m) e -> p m u e", u=PACK)[:, rows],
-                                    prod[s][:].rearrange("p e (m u) -> p m u e", u=PACK)[:, rows],
-                                    picked_a[s][:].rearrange("p e (m u) -> p m u e", u=PACK)[:, rows], ALU.subtract)
+            m_range = slice(lo // PACK, hi // PACK)
+            nc.vector.tensor_tensor(z_pairs[:, s].rearrange("p (u m) e -> p m u e", u=PACK)[:, m_range],
+                                    gated_a[s][:].rearrange("p e (m u) -> p m u e", u=PACK)[:, m_range],
+                                    picked_a[s][:].rearrange("p e (m u) -> p m u e", u=PACK)[:, m_range], ALU.subtract)
 
-        def z_single(t, lo, hi):
-            rows = slice(lo // PACK, hi // PACK)
-            nc.vector.tensor_tensor(z_pairs[:, t // 2, :, t % 2].rearrange("p (u m) -> p m u", u=PACK)[:, rows],
-                                    prod[t // 2][:, t % 2, :].rearrange("p (m u) -> p m u", u=PACK)[:, rows],
-                                    picked_a[t // 2][:, t % 2, :].rearrange("p (m u) -> p m u", u=PACK)[:, rows], ALU.subtract)
-
-        def weave(name, pairs, lo, hi, engine=nc.vector):
-            grouped = sb(name, [P, (hi - lo) * PACK], BF16)
+        def weave(engine, name, pairs, cols):
+            grouped = sb(name, [P, (cols.stop - cols.start) * PACK], BF16)
             words = pairs[:].rearrange("p s c e -> p s (c e)").bitcast(I32)
             engine.tensor_copy(grouped[:].bitcast(I32).rearrange("p (c s) -> p c s", s=2),
-                                  words[:, :, lo:hi].rearrange("p s c -> p c s"))
+                               words[:, :, cols].rearrange("p s c -> p c s"))
             return grouped
 
-        project(b_ps, (xb_w, xb_s), wb_q)
-        fetch_gate(0, nc.scalar.copy, "wa_raw0")
-        fetch_gate(1, nc.vector.tensor_copy)
-        quantize_half(wa_q, 0, wa_g[0][:])
-        fetch_gate(2, nc.vector.tensor_copy)
-        quantize_half(wa_q, 1, wa_g[1][:])
-        project(a_ps, (xa_w, xa_s), wa_q)
-        fetch_gate(3, nc.vector.tensor_copy, "wa_g1")
+        def quantized(name, grouped, width):
+            operand = planes(name, width)
+            quantize(operand, slice(0, width), grouped[:])
+            return operand
+
+        b_tile(0, nc.scalar.copy, after="wa_raw0")
+        quantize(wa_q, halves[0], wa_g[0][:])
+        b_tile(1, nc.vector.tensor_copy, after="wa_g0")
+        b_tile(2, nc.vector.tensor_copy)
+        quantize(wa_q, halves[1], wa_g[1][:])
+        for t in range(PACK):
+            mx(a_ps[t][:], xa_q, row_tiles[t], wa_q, all_cols)
+        b_tile(3, nc.vector.tensor_copy, after="wa_g1")
+
         for s in range(2):
             for t in (2 * s, 2 * s + 1):
-                half_a(t)
+                nc.vector.tensor_scalar(half_a[t][:, :H], a_ps[t][:], gt_sb[:, t:t + 1], 0.5, ALU.mult, ALU.mult)
             for t in (2 * s, 2 * s + 1):
-                gated(t)
-        z2_q = quantize("zb", weave("z2_g", z2_pairs, 0, H, nc.gpsimd), H)
+                nc.vector.scalar_tensor_tensor(gated_a[s][:, t % 2, :], a_ps[t][:], gt_sb[:, t:t + 1], b_gate[t][:],
+                                               ALU.mult, ALU.mult)
+        z2_q = quantized("z2", weave(nc.gpsimd, "z2_g", z2_pairs, all_cols), H)
         for t in (0, 1):
             fetch_a(t, 0, H)
         z_pair(0, 0, H)
-        for t, cuts in ((2, (0, H)), (3, (0, H - QUARTER, H))):
-            for lo, hi in zip(cuts, cuts[1:]):
-                fetch_a(t, lo, hi)
-                z_single(t, lo, hi)
+        fetch_a(2, 0, H)
+        for lo in range(0, H, QUARTER):
+            fetch_a(3, lo, lo + QUARTER)
+            z_pair(1, lo, lo + QUARTER)
 
         cv = [sb("cv%d" % u, [P, H], F32) for u in range(PACK)]
         y = [sb("y%d" % u, [P, H], F32) for u in range(PACK)]
         pa = [sb("pa%d" % u, [P, W], F32) for u in range(PACK)]
-        gate = [sb("gate%d" % u, [P, W], F32) for u in range(PACK)]
+        pb_gate = [sb("pb_gate%d" % u, [P, W], F32) for u in range(PACK)]
         ra = [sb("ra%d" % u, [P, W], F32) for u in range(PACK)]
         y_g = [sb("y_g%d" % h, [P, HALF, PACK], BF16) for h in range(2)]
         out_rows = out_0.rearrange("(p u) c -> p u c", u=PACK)
 
-        z_g = [weave("z_g%d" % u, z_pairs, u * P, (u + 1) * P) for u in range(2)]
-        z_q = quantize("za0", z_g[0], P)
-        mx(b_ps[0][:, :HALF], z_q, slice(0, P), z2_q, slice(0, HALF))
-        mx(a_ps[0][:, :HALF], z_q, slice(0, P), z2_q, slice(HALF, H))
-        nc.scalar.activation(cv[0][:, :HALF], b_ps[0][:, :HALF], ACT.Copy, scale=0.0625)
-        nc.scalar.activation(cv[0][:, HALF:], a_ps[0][:, :HALF], ACT.Copy, scale=0.0625)
+        z_g = [weave(nc.vector, "z_g%d" % u, z_pairs, row_tiles[u]) for u in range(2)]
+        z_first = quantized("z_tile0", z_g[0], P)
+        first_banks = (banks[0], banks[PACK])
+        for h in range(2):
+            mx(first_banks[h][:, :HALF], z_first, slice(0, P), z2_q, halves[h])
+        for h in range(2):
+            nc.scalar.activation(cv[0][:, halves[h]], first_banks[h][:, :HALF], ACT.Copy, scale=CV_SCALE)
         for u in range(1, PACK):
             if u + 1 < PACK:
-                z_g.append(weave("z_g%d" % (u + 1), z_pairs, (u + 1) * P, (u + 2) * P))
-            mx(b_ps[u][:], quantize("za%d" % u, z_g[u], P), slice(0, P), z2_q, slice(0, H))
-            nc.vector.tensor_scalar(cv[u][:], b_ps[u][:], 0.0625, None, ALU.mult)
+                z_g.append(weave(nc.vector, "z_g%d" % (u + 1), z_pairs, row_tiles[u + 1]))
+            mx(banks[u][:], quantized("z_tile%d" % u, z_g[u], P), slice(0, P), z2_q, all_cols)
+            nc.vector.tensor_scalar(cv[u][:], banks[u][:], CV_SCALE, None, ALU.mult)
+
         for u in range(PACK):
-            nc.scalar.activation(gate[u][:], cv[u][:].indirect(n4_l[:]), ACT.Sigmoid)
+            nc.scalar.activation(pb_gate[u][:], cv[u][:].indirect(n4_l[:]), ACT.Sigmoid)
             nc.scalar.activation(pa[u][:], cv[u][:].indirect(n3_l[:]), ACT.Copy)
             nc.vector.tensor_copy(y[u][:], cv[u][:])
-            nc.vector.tensor_tensor(ra[u][:], pa[u][:], gate[u][:], ALU.mult)
+            nc.vector.tensor_tensor(ra[u][:], pa[u][:], pb_gate[u][:], ALU.mult)
         for u in range(PACK):
             nc.scalar.activation(y[u][:].indirect(n4_l[:]), ra[u][:], ACT.Copy)
             nc.sync.dma_start(out_rows[:, u, :], y[u][:])
             for h in range(2):
-                nc.vector.tensor_copy(y_g[h][:, :, u], y[u][:, h * HALF:(h + 1) * HALF])
+                nc.vector.tensor_copy(y_g[h][:, :, u], y[u][:, halves[h]])
 
-        y_codes = sb("y_codes", [P, H], U32)
-        y_scales = sb("y_scales", [P, H], U8)
+        y_q = planes("y", H)
         out_words = out_1[0].rearrange("p c r -> p (c r)").bitcast(I32)
         for h in range(2):
-            cols = slice(h * HALF, (h + 1) * HALF)
-            nc.vector.quantize_mx(out=y_codes[:, cols].bitcast(FP8X4), scales=y_scales[:, cols],
-                                  in_=y_g[h][:].rearrange("p c u -> p (c u)"))
-            nc.sync.dma_start(out_words[:, cols], y_codes[:, cols].bitcast(I32))
-        for q in range(4):
-            (nc.scalar, nc.sync)[q % 2].dma_start(out_2[0, 4 * q:4 * q + 4, :].bitcast(I32), y_scales[32 * q:32 * q + 4, :].bitcast(I32))
+            quantize(y_q, halves[h], y_g[h][:].rearrange("p c u -> p (c u)"))
+            nc.sync.dma_start(out_words[:, halves[h]], y_q[0][:, halves[h]].bitcast(I32))
+        for q in range(QUADRANTS):
+            queue = (nc.scalar, nc.sync)[q % 2]
+            queue.dma_start(out_2[0, 4 * q:4 * q + 4, :].bitcast(I32), y_q[1][32 * q:32 * q + 4, :].bitcast(I32))

@@ -21,10 +21,10 @@ QUADRANTS = 4
 HALF = H // 2
 QUARTER = H // 4
 LIST_ROWS = 16
-WA_PIECES = ((0, QUARTER), (QUARTER, HALF), (HALF, H))
 A_WINDOW = H + 16
 B_WINDOW = 2 * H
 CV_SCALE = 0.0625
+B_BANKS = (0, 1, 0, 0)
 
 
 def tile_picked_momtgatebfold_none_po_kernel(
@@ -47,8 +47,9 @@ def tile_picked_momtgatebfold_none_po_kernel(
             nc.sync.dma_start(raw[:], w.rearrange("(p j) c -> p j c", j=PACK)[:, :, lo:hi])
             return raw
 
-        def round_weights(copy, grouped, raw):
-            copy(grouped.rearrange("p (c i j) -> p c j i", i=4, j=PACK), raw[:].rearrange("p j (c i) -> p c j i", i=4))
+        def round_on_scalar(grouped, raw):
+            nc.scalar.copy(grouped.rearrange("p (c i j) -> p c j i", i=4, j=PACK),
+                           raw[:].rearrange("p j (c i) -> p c j i", i=4))
 
         def planes(name, width, after=None):
             return sb(name + "_codes", [P, width], U32, after), sb(name + "_scales", [P, width], U8)
@@ -75,7 +76,8 @@ def tile_picked_momtgatebfold_none_po_kernel(
         wb_raw.append(load_columns("wb_raw1", wb, HALF, H))
         nc.sync.dma_start(x_codes[:].bitcast(I32), x_words[0].rearrange("p c r -> p (c r)").bitcast(I32))
         n2_l = load_list("n2_l", n2)
-        wa_raw = [load_columns("wa_raw%d" % i, wa, lo, hi) for i, (lo, hi) in enumerate(WA_PIECES)]
+        wa_raw = [load_columns("wa_raw0", wa, 0, QUARTER), load_columns("wa_raw1", wa, QUARTER, HALF),
+                  load_columns("wa_raw2", wa, HALF, H)]
         gt_sb = sb("gt_sb", [P, PACK], F32)
         gi_sb = sb("gi_sb", [P, PACK], F32)
         nc.sync.dma_start(gi_sb[:], gi.rearrange("(p t) o -> p (t o)", t=PACK))
@@ -98,16 +100,15 @@ def tile_picked_momtgatebfold_none_po_kernel(
         wb_q = planes("wb", H, after="x_bytes")
         for h in range(2):
             wb_g = sb("wb_g%d" % h, [P, HALF * PACK], BF16)
-            round_weights(nc.scalar.copy, wb_g[:], wb_raw[h])
+            round_on_scalar(wb_g[:], wb_raw[h])
             quantize(wb_q, halves[h], wb_g[:])
         xb_q = (pick("xb_codes", x_codes, two_l, U32), xb_bytes)
         xa_q = (pick("xa_codes", x_codes, offs_l, U32), xa_bytes)
-        wa_q = planes("wa", H)
-        wa_g = [sb("wa_g%d" % h, [P, HALF * PACK], BF16) for h in range(2)]
-        round_weights(nc.scalar.copy, wa_g[0][:, :QUARTER * PACK], wa_raw[0])
-        round_weights(nc.vector.tensor_copy, wa_g[0][:, QUARTER * PACK:], wa_raw[1])
-        nc.gpsimd.tensor_scalar(wa_g[1][:].rearrange("p (c j) -> p c j", j=PACK), wa_raw[2][:].rearrange("p j c -> p c j"),
-                                1.0, 0.0, ALU.mult, ALU.add)
+        wa_g = sb("wa_g", [P, H * PACK], BF16)
+        round_on_scalar(wa_g[:, :QUARTER * PACK], wa_raw[0])
+        round_on_scalar(wa_g[:, QUARTER * PACK:HALF * PACK], wa_raw[1])
+        nc.gpsimd.tensor_scalar(wa_g[:, HALF * PACK:].rearrange("p (c j) -> p c j", j=PACK),
+                                wa_raw[2][:].rearrange("p j c -> p c j"), 1.0, 0.0, ALU.mult, ALU.add)
 
         banks = [psum.tile([P, H], F32, name="bank%d" % i) for i in range(2 * PACK)]
         a_ps = banks[PACK:]
@@ -118,14 +119,12 @@ def tile_picked_momtgatebfold_none_po_kernel(
         gated_a = [sb("gated_a%d" % s, [P, 2, H], F32) for s in range(2)]
         picked_a = [sb("picked_a%d" % s, [P, 2, H], F32) for s in range(2)]
         z_pairs = sb("z_pairs", [P, 2, H, 2], BF16)
-        z2_pairs = sb("z2_pairs", [P, 2, H, 2], BF16)
 
         def b_tile(t, copy, after=None):
             b_sb.append(sb("b_sb%d" % t, [P, B_WINDOW], F32, after))
-            mx(banks[t % 2][:], xb_q, row_tiles[t], wb_q, all_cols)
-            copy(b_sb[t][:, :H], banks[t % 2][:])
+            mx(banks[B_BANKS[t]][:], xb_q, row_tiles[t], wb_q, all_cols)
+            copy(b_sb[t][:, :H], banks[B_BANKS[t]][:])
             nc.scalar.activation(b_gate[t][:], b_sb[t][:].indirect(n2_l[:]), ACT.Sigmoid)
-            nc.gpsimd.tensor_scalar(z2_pairs[:, t // 2, :, t % 2], b_sb[t][:, :H], gi_sb[:, t:t + 1], 0.0, ALU.mult, ALU.add)
 
         def fetch_a(t, lo, hi):
             nc.scalar.activation(picked_a[t // 2][:, t % 2, lo:hi],
@@ -150,13 +149,15 @@ def tile_picked_momtgatebfold_none_po_kernel(
             return operand
 
         b_tile(0, nc.scalar.copy, after="wa_raw0")
-        quantize(wa_q, halves[0], wa_g[0][:])
-        b_tile(1, nc.vector.tensor_copy, after="wa_g0")
+        b_tile(1, nc.vector.tensor_copy, after="wa_raw1")
         b_tile(2, nc.vector.tensor_copy)
-        quantize(wa_q, halves[1], wa_g[1][:])
+        wa_q = quantized("wa", wa_g, H)
         for t in range(PACK):
             mx(a_ps[t][:], xa_q, row_tiles[t], wa_q, all_cols)
-        b_tile(3, nc.vector.tensor_copy, after="wa_g1")
+        b_tile(3, nc.vector.tensor_copy)
+        z2_pairs = sb("z2_pairs", [P, 2, H, 2], BF16, after="wa_g")
+        for t in range(PACK):
+            nc.gpsimd.tensor_scalar(z2_pairs[:, t // 2, :, t % 2], b_sb[t][:, :H], gi_sb[:, t:t + 1], 0.0, ALU.mult, ALU.add)
 
         for s in range(2):
             for t in (2 * s, 2 * s + 1):

from contextlib import ExitStack

import concourse.mybir as mybir

T, S, H, W = 2048, 512, 512, 256
FLOPS = 3 * 2 * 512 * 512 * 512

F32 = mybir.dt.float32
BF16 = mybir.dt.bfloat16
I32 = mybir.dt.int32
U32 = mybir.dt.uint32
U16 = mybir.dt.uint16
U8 = mybir.dt.uint8
FP8X4 = mybir.dt.float8_e4m3fn_x4
ALU = mybir.AluOpType
ACT = mybir.ActivationFunctionType

P = 128
PACK = 4
QUADRANTS = 4
HALF = H // 2
QUARTER = H // 4
LIST_ROWS = 16
A_WINDOW = H + 16
B_WINDOW = 2 * H
CV_SCALE = 0.0625
B_BANKS = (0, 1, 0, 0)


def tile_picked_momtgatebfold_none_po_kernel(
        tc, x_words, x_scales, wa, wb, gt, gi, offs, two, n1, n2, n3, n4, out_0, out_1, out_2):
    nc = tc.nc
    with ExitStack() as ctx:
        keep = ctx.enter_context(tc.tile_pool(name="keep", bufs=1))
        psum = ctx.enter_context(tc.psum_pool(name="psum", bufs=1))

        def sb(name, shape, dtype, after=None):
            return keep.tile(shape, dtype, name=name, tag=after or name, align_bytes=64)

        def load_list(name, src):
            tile = keep.tile(list(src.shape), U16, name=name)
            nc.sync.dma_start(tile[:], src)
            return tile

        def load_columns(name, w, lo, hi):
            raw = sb(name, [P, PACK, hi - lo], F32)
            nc.sync.dma_start(raw[:], w.rearrange("(p j) c -> p j c", j=PACK)[:, :, lo:hi])
            return raw

        def round_on_scalar(grouped, raw):
            nc.scalar.copy(grouped.rearrange("p (c i j) -> p c j i", i=4, j=PACK),
                           raw[:].rearrange("p j (c i) -> p c j i", i=4))

        def planes(name, width, after=None):
            return sb(name + "_codes", [P, width], U32, after), sb(name + "_scales", [P, width], U8)

        def quantize(operand, cols, grouped):
            nc.vector.quantize_mx(out=operand[0][:, cols].bitcast(FP8X4), scales=operand[1][:, cols], in_=grouped)

        def mx(out, lhs, lhs_cols, rhs, rhs_cols):
            nc.tensor.matmul_mx(out=out, lhsT=lhs[0][:, lhs_cols].bitcast(FP8X4), lhsT_scale=lhs[1][:, lhs_cols],
                                rhs=rhs[0][:, rhs_cols].bitcast(FP8X4), rhs_scale=rhs[1][:, rhs_cols], start=True, stop=True)

        halves = [slice(0, HALF), slice(HALF, H)]
        row_tiles = [slice(t * P, (t + 1) * P) for t in range(PACK)]
        all_cols = slice(0, H)

        x_codes = sb("x_codes", [P, T], U32)
        x_bytes = sb("x_bytes", [P, T], U8)
        nc.vector.memset(x_bytes[:].bitcast(I32), 0)
        two_l = load_list("two_l", two)
        offs_l = load_list("offs_l", offs)
        wb_raw = [load_columns("wb_raw0", wb, 0, HALF)]
        for q in range(QUADRANTS):
            nc.sync.dma_start(x_bytes[32 * q:32 * q + 4, :].bitcast(I32), x_scales[0, 4 * q:4 * q + 4, :].bitcast(I32))
        wb_raw.append(load_columns("wb_raw1", wb, HALF, H))
        nc.sync.dma_start(x_codes[:].bitcast(I32), x_words[0].rearrange("p c r -> p (c r)").bitcast(I32))
        n2_l = load_list("n2_l", n2)
        wa_raw = [load_columns("wa_raw0", wa, 0, QUARTER), load_columns("wa_raw1", wa, QUARTER, HALF),
                  load_columns("wa_raw2", wa, HALF, H)]
        gt_sb = sb("gt_sb", [P, PACK], F32)
        gi_sb = sb("gi_sb", [P, PACK], F32)
        nc.sync.dma_start(gi_sb[:], gi.rearrange("(p t) o -> p (t o)", t=PACK))
        nc.sync.dma_start(gt_sb[:], gt.rearrange("(p t) o -> p (t o)", t=PACK))
        n1_l = load_list("n1_l", n1)
        n4_l = load_list("n4_l", n4)
        n3_l = load_list("n3_l", n3)

        warm = sb("warm", [P, 2], F32)
        nc.vector.memset(warm[:, 0:1], 0.0)
        nc.scalar.activation(warm[:, 1:2], warm[:, 0:1], ACT.Sigmoid)

        def pick(name, window, entries, dtype):
            picked = sb(name, [P, S], dtype)
            nc.vector.tensor_copy(picked[:].rearrange("p (t m) -> p m t", t=PACK), window[:].indirect(entries[:]))
            return picked

        xb_bytes = pick("xb_bytes", x_bytes, two_l, U8)
        xa_bytes = pick("xa_bytes", x_bytes, offs_l, U8)
        wb_q = planes("wb", H, after="x_bytes")
        for h in range(2):
            wb_g = sb("wb_g%d" % h, [P, HALF * PACK], BF16)
            round_on_scalar(wb_g[:], wb_raw[h])
            quantize(wb_q, halves[h], wb_g[:])
        xb_q = (pick("xb_codes", x_codes, two_l, U32), xb_bytes)
        xa_q = (pick("xa_codes", x_codes, offs_l, U32), xa_bytes)
        wa_g = sb("wa_g", [P, H * PACK], BF16)
        round_on_scalar(wa_g[:, :QUARTER * PACK], wa_raw[0])
        round_on_scalar(wa_g[:, QUARTER * PACK:HALF * PACK], wa_raw[1])
        nc.gpsimd.tensor_scalar(wa_g[:, HALF * PACK:].rearrange("p (c j) -> p c j", j=PACK),
                                wa_raw[2][:].rearrange("p j c -> p c j"), 1.0, 0.0, ALU.mult, ALU.add)

        banks = [psum.tile([P, H], F32, name="bank%d" % i) for i in range(2 * PACK)]
        a_ps = banks[PACK:]

        b_sb = []
        half_a = [sb("half_a%d" % t, [P, A_WINDOW], F32) for t in range(PACK)]
        b_gate = [sb("b_gate%d" % t, [P, H], F32) for t in range(PACK)]
        gated_a = [sb("gated_a%d" % s, [P, 2, H], F32) for s in range(2)]
        picked_a = [sb("picked_a%d" % s, [P, 2, H], F32) for s in range(2)]
        z_pairs = sb("z_pairs", [P, 2, H, 2], BF16)

        def b_tile(t, copy, after=None):
            b_sb.append(sb("b_sb%d" % t, [P, B_WINDOW], F32, after))
            mx(banks[B_BANKS[t]][:], xb_q, row_tiles[t], wb_q, all_cols)
            copy(b_sb[t][:, :H], banks[B_BANKS[t]][:])
            nc.scalar.activation(b_gate[t][:], b_sb[t][:].indirect(n2_l[:]), ACT.Sigmoid)

        def fetch_a(t, lo, hi):
            nc.scalar.activation(picked_a[t // 2][:, t % 2, lo:hi],
                                 half_a[t][:].indirect(n1_l[:, lo // LIST_ROWS:hi // LIST_ROWS]), ACT.Copy)

        def z_pair(s, lo, hi):
            m_range = slice(lo // PACK, hi // PACK)
            nc.vector.tensor_tensor(z_pairs[:, s].rearrange("p (u m) e -> p m u e", u=PACK)[:, m_range],
                                    gated_a[s][:].rearrange("p e (m u) -> p m u e", u=PACK)[:, m_range],
                                    picked_a[s][:].rearrange("p e (m u) -> p m u e", u=PACK)[:, m_range], ALU.subtract)

        def weave(engine, name, pairs, cols):
            grouped = sb(name, [P, (cols.stop - cols.start) * PACK], BF16)
            words = pairs[:].rearrange("p s c e -> p s (c e)").bitcast(I32)
            engine.tensor_copy(grouped[:].bitcast(I32).rearrange("p (c s) -> p c s", s=2),
                               words[:, :, cols].rearrange("p s c -> p c s"))
            return grouped

        def quantized(name, grouped, width):
            operand = planes(name, width)
            quantize(operand, slice(0, width), grouped[:])
            return operand

        b_tile(0, nc.scalar.copy, after="wa_raw0")
        b_tile(1, nc.vector.tensor_copy, after="wa_raw1")
        b_tile(2, nc.vector.tensor_copy)
        wa_q = quantized("wa", wa_g, H)
        for t in range(PACK):
            mx(a_ps[t][:], xa_q, row_tiles[t], wa_q, all_cols)
        b_tile(3, nc.vector.tensor_copy)
        z2_pairs = sb("z2_pairs", [P, 2, H, 2], BF16, after="wa_g")
        for t in range(PACK):
            nc.gpsimd.tensor_scalar(z2_pairs[:, t // 2, :, t % 2], b_sb[t][:, :H], gi_sb[:, t:t + 1], 0.0, ALU.mult, ALU.add)

        for s in range(2):
            for t in (2 * s, 2 * s + 1):
                nc.vector.tensor_scalar(half_a[t][:, :H], a_ps[t][:], gt_sb[:, t:t + 1], 0.5, ALU.mult, ALU.mult)
            for t in (2 * s, 2 * s + 1):
                nc.vector.scalar_tensor_tensor(gated_a[s][:, t % 2, :], a_ps[t][:], gt_sb[:, t:t + 1], b_gate[t][:],
                                               ALU.mult, ALU.mult)
        z2_q = quantized("z2", weave(nc.gpsimd, "z2_g", z2_pairs, all_cols), H)
        for t in (0, 1):
            fetch_a(t, 0, H)
        z_pair(0, 0, H)
        fetch_a(2, 0, H)
        for lo in range(0, H, QUARTER):
            fetch_a(3, lo, lo + QUARTER)
            z_pair(1, lo, lo + QUARTER)

        cv = [sb("cv%d" % u, [P, H], F32) for u in range(PACK)]
        y = [sb("y%d" % u, [P, H], F32) for u in range(PACK)]
        pa = [sb("pa%d" % u, [P, W], F32) for u in range(PACK)]
        pb_gate = [sb("pb_gate%d" % u, [P, W], F32) for u in range(PACK)]
        ra = [sb("ra%d" % u, [P, W], F32) for u in range(PACK)]
        y_g = [sb("y_g%d" % h, [P, HALF, PACK], BF16) for h in range(2)]
        out_rows = out_0.rearrange("(p u) c -> p u c", u=PACK)

        z_g = [weave(nc.vector, "z_g%d" % u, z_pairs, row_tiles[u]) for u in range(2)]
        z_first = quantized("z_tile0", z_g[0], P)
        first_banks = (banks[0], banks[PACK])
        for h in range(2):
            mx(first_banks[h][:, :HALF], z_first, slice(0, P), z2_q, halves[h])
        for h in range(2):
            nc.scalar.activation(cv[0][:, halves[h]], first_banks[h][:, :HALF], ACT.Copy, scale=CV_SCALE)
        for u in range(1, PACK):
            if u + 1 < PACK:
                z_g.append(weave(nc.vector, "z_g%d" % (u + 1), z_pairs, row_tiles[u + 1]))
            mx(banks[u][:], quantized("z_tile%d" % u, z_g[u], P), slice(0, P), z2_q, all_cols)
            nc.vector.tensor_scalar(cv[u][:], banks[u][:], CV_SCALE, None, ALU.mult)

        for u in range(PACK):
            nc.scalar.activation(pb_gate[u][:], cv[u][:].indirect(n4_l[:]), ACT.Sigmoid)
            nc.scalar.activation(pa[u][:], cv[u][:].indirect(n3_l[:]), ACT.Copy)
            nc.vector.tensor_copy(y[u][:], cv[u][:])
            nc.vector.tensor_tensor(ra[u][:], pa[u][:], pb_gate[u][:], ALU.mult)
        for u in range(PACK):
            nc.scalar.activation(y[u][:].indirect(n4_l[:]), ra[u][:], ACT.Copy)
            nc.sync.dma_start(out_rows[:, u, :], y[u][:])
            for h in range(2):
                nc.vector.tensor_copy(y_g[h][:, :, u], y[u][:, halves[h]])

        y_q = planes("y", H)
        out_words = out_1[0].rearrange("p c r -> p (c r)").bitcast(I32)
        for h in range(2):
            quantize(y_q, halves[h], y_g[h][:].rearrange("p c u -> p (c u)"))
            nc.sync.dma_start(out_words[:, halves[h]], y_q[0][:, halves[h]].bitcast(I32))
        for q in range(QUADRANTS):
            queue = (nc.scalar, nc.sync)[q % 2]
            queue.dma_start(out_2[0, 4 * q:4 * q + 4, :].bitcast(I32), y_q[1][32 * q:32 * q + 4, :].bitcast(I32))
